import numpy as np
import ml_dtypes


def mxq(x, axis, fmt="e4m3"):
    dtype, down = {"e4m3": (ml_dtypes.float8_e4m3fn, 7), "e5m2": (ml_dtypes.float8_e5m2, 14)}[fmt]
    v = np.moveaxis(np.asarray(x, np.float32).astype(ml_dtypes.bfloat16).astype(np.float64), axis, -1)
    blocks = v.reshape(v.shape[:-1] + (-1, 32))
    amax = np.abs(blocks).max(-1, keepdims=True)
    byte = np.maximum(np.where(amax > 0, np.frexp(amax)[1] - 1 + 127, 0) - down, 1)
    scale = np.exp2(byte - 127.0)
    codes = (blocks / scale).astype(np.float32).astype(dtype).astype(np.float64)
    return np.moveaxis((codes * scale).reshape(v.shape), -1, axis)


WIDE = False


def mx_kscale(k):
    if not WIDE:
        return np.ones(k)
    levels = np.array([10, -10, 5, -5, 0])
    if k % 512:
        return np.exp2(np.random.permutation(np.resize(levels, k // 32))).repeat(32)
    a = np.empty((k // 512, 16))
    for p in range(k // 512):
        a[p, :8] = np.random.permutation(np.resize(levels, 8))
        for g in range(8):
            far = levels[np.abs(levels - a[p, g]) >= 10]
            a[p, g + 8] = far[np.random.randint(len(far))]
    return np.exp2(a.ravel()).repeat(32)


def f64(x):
    return np.asarray(x).astype(np.float64)


def striped(idx):
    return np.tile(np.asarray(idx).reshape(-1, 16).T, (8, 1)).astype(np.uint16)


def unstriped(offs):
    return offs[:16].T.reshape(-1).astype(np.int64)


E2M1 = np.array([0.0, 0.5, 1.0, 1.5, 2.0, 3.0, 4.0, 6.0, -0.0, -0.5, -1.0, -1.5, -2.0, -3.0, -4.0, -6.0])


def pack_weight(w, fmt):
    k, n = w.shape
    w = f64(np.asarray(w, np.float32).astype(ml_dtypes.bfloat16)).reshape(k // 32, 32, n)
    amax = np.abs(w).max(1)
    if fmt == "e4m3":
        byte = np.frexp(amax)[1] - 1 + 127 - 7
    else:
        mant, ex = np.frexp(amax / 6.0)
        byte = np.where(mant > 0.5, ex, ex - 1) + 127
    byte = np.clip(np.where(amax > 0, byte, 1), 1, 254)
    scaled = (w * np.exp2(127.0 - byte)[:, None, :]).reshape(k, n).astype(np.float32)
    by_word = np.ascontiguousarray(scaled.reshape(k // 512, 128, 4, n).transpose(0, 1, 3, 2))
    if fmt == "e4m3":
        words = by_word.astype(ml_dtypes.float8_e4m3fn).view(np.uint8)
    else:
        c = by_word.astype(ml_dtypes.float4_e2m1fn).view(np.uint8) & 0xF
        words = (c[..., 0::2] | (c[..., 1::2] << 4)).reshape(k // 512, 128, 2 * n)
    return np.ascontiguousarray(words), np.ascontiguousarray(byte.astype(np.uint8).reshape(k // 512, 16, n))


def unpack_weight(words, scales, fmt):
    g, _, n = scales.shape
    words = np.ascontiguousarray(words).reshape(g, 128, n, -1)
    if fmt == "e4m3":
        vals = words.view(ml_dtypes.float8_e4m3fn).astype(np.float64)
    else:
        nib = np.empty((g, 128, n, 4), np.uint8)
        nib[..., 0::2] = words & 0xF
        nib[..., 1::2] = words >> 4
        vals = E2M1[nib]
    vals = vals * np.repeat(np.exp2(scales.astype(np.float64) - 127.0), 8, axis=1)[..., None]
    return vals.transpose(0, 1, 3, 2).reshape(g * 512, n)


def bf(x):
    return np.asarray(x, np.float32).astype(ml_dtypes.bfloat16)


def planes(Y):
    r, m = Y.shape
    b = f64(bf(Y)).reshape(r // 32, 32, m)
    amax = np.abs(b).max(1)
    byte = np.clip(np.where(amax > 0, np.frexp(amax)[1] - 1 + 127 - 7, 1), 1, 254)
    codes = (b * np.exp2(127.0 - byte)[:, None, :]).reshape(r, m).astype(np.float32).astype(ml_dtypes.float8_e4m3fn).view(np.uint8)
    words = codes.reshape(r // 512, 128, 4, m).transpose(0, 1, 3, 2)
    return np.ascontiguousarray(words), np.ascontiguousarray(byte.astype(np.uint8).reshape(r // 512, 16, m))


K, I, L, S, T, N, M = 1024, 512, 512, 512, 512, 512, 512


def setup_inputs():
    n = np.random.standard_normal
    idx = np.random.randint(0, I, T)
    idx2 = np.random.randint(0, S, T)
    fk = mx_kscale(K)
    fn = mx_kscale(N)
    fl = mx_kscale(L)
    xap = pack_weight(n((K, I)) / fk[:, None], "e2m1")
    wap = pack_weight(n((K, N)) * 1 / np.sqrt(K) * fk[:, None] * fn, "e4m3")
    xbp = pack_weight(n((L, S)) / fl[:, None], "e4m3")
    wbp = pack_weight(n((L, N)) * 1 / np.sqrt(L) * fl[:, None] * fn, "e2m1")
    wmp = pack_weight(n((N, M)) * 1 / np.sqrt(N) / fn[:, None], "e4m3")
    return {
        "xa_words": xap[0],
        "xa_scales": xap[1],
        "wa_words": wap[0],
        "wa_scales": wap[1],
        "xb_words": xbp[0],
        "xb_scales": xbp[1],
        "wb_words": wbp[0],
        "wb_scales": wbp[1],
        "wm_words": wmp[0],
        "wm_scales": wmp[1],
        "offs": striped(idx),
        "offs2": striped(idx2),
    }


def reference(xa_words, xa_scales, wa_words, wa_scales, xb_words, xb_scales, wb_words, wb_scales, wm_words, wm_scales, offs, offs2):
    idx = unstriped(offs)
    idx2 = unstriped(offs2)
    xau = unpack_weight(xa_words, xa_scales, "e2m1")
    wau = unpack_weight(wa_words, wa_scales, "e4m3")
    xbu = unpack_weight(xb_words, xb_scales, "e4m3")
    wbu = unpack_weight(wb_words, wb_scales, "e2m1")
    wmu = unpack_weight(wm_words, wm_scales, "e4m3")
    za = wau.T @ xau
    zb = wbu.T @ xbu
    h1 = np.maximum(za[:, idx] + zb[:, idx2], 0.0)
    h1q = mxq(h1, 0, "e4m3")
    y = wmu.T @ h1q
    words, scales = planes(y)
    return y, words, scales

@@ -1,0 +1,240 @@
+from contextlib import ExitStack
+
+import concourse.mybir as mybir
+
+F32 = mybir.dt.float32
+BF16 = mybir.dt.bfloat16
+I32 = mybir.dt.int32
+U32 = mybir.dt.uint32
+U16 = mybir.dt.uint16
+U8 = mybir.dt.uint8
+FP8X4 = mybir.dt.float8_e4m3fn_x4
+FP4X4 = mybir.dt.float4_e2m1fn_x4
+RELU = mybir.ActivationFunctionType.Relu
+ADD = mybir.AluOpType.add
+
+P = 128
+PACK = 4
+W = 512
+QUADS = 4
+LIST_ROWS = 16
+HALF = 256
+STEP = 128
+
+FLOPS = 2 * (1024 * 512 * 512 + 512 * 512 * 512 + 512 * 512 * 512)
+
+
+def load_scale_rows(queue, plane, scales, quad):
+    queue.dma_start(
+        out=plane[32 * quad : 32 * quad + 4].bitcast(I32),
+        in_=scales[:, 4 * quad : 4 * quad + 4, :].rearrange("g q c -> q g c").bitcast(I32),
+    )
+
+
+def load_scale_rows_spread(queue, plane, scales, row):
+    queue.dma_start(
+        out=plane[row:P:4, 0, :].bitcast(I32),
+        in_=scales[0, row:16:4, :].bitcast(I32).unsqueeze(1).to_broadcast([QUADS, 8, W // 4]),
+    )
+
+
+def deal(engine, dealt, raw):
+    engine.tensor_copy(
+        out=dealt.rearrange("p g (r m) -> p g r m", r=PACK),
+        in_=raw.rearrange("p g (m r) -> p g r m", r=PACK),
+    )
+
+
+def tile_moe_combined_hidden_next_layer_pl_kernel(
+    tc, xa_words, xa_scales, wa_words, wa_scales, xb_words, xb_scales, wb_words, wb_scales,
+    wm_words, wm_scales, offs, offs2, out_0, out_1, out_2,
+):
+    nc = tc.nc
+    with ExitStack() as ctx:
+        lists = ctx.enter_context(tc.tile_pool(name="lists", bufs=1))
+        keep = ctx.enter_context(tc.tile_pool(name="keep", bufs=1))
+        psum = ctx.enter_context(tc.psum_pool(name="psum", bufs=1))
+
+        idx_a = lists.tile([P, W // LIST_ROWS], U16, name="idx_a")
+        idx_b = lists.tile([P, W // LIST_ROWS], U16, name="idx_b")
+
+        wb_raw = keep.tile([P, 2 * W], U8, name="wb_raw", align_bytes=64)
+        wb_w = keep.tile([P, 2 * W], U8, name="wb_w", align_bytes=64)
+        wb_sraw = keep.tile([P, 1, W], U8, name="wb_sraw", align_bytes=64)
+        wb_s = keep.tile([P, W], U8, name="wb_s", align_bytes=64)
+        xb_w = keep.tile([P, W], I32, name="xb_w", align_bytes=64)
+        xb_s = keep.tile([P, 1, W], U8, name="xb_s", align_bytes=64)
+        wa_raw = keep.tile([P, 2, W], I32, name="wa_raw", tag="picked_late", align_bytes=64)
+        wa_w = keep.tile([P, 2, W], I32, name="wa_w", align_bytes=64)
+        wa_sraw = keep.tile([P, 2, W], U8, name="wa_sraw", tag="picked_early", align_bytes=64)
+        wa_s = keep.tile([P, 2, W], U8, name="wa_s", align_bytes=64)
+        xa_w = keep.tile([P, 2, 2 * W], U8, name="xa_w", align_bytes=64)
+        xa_s = keep.tile([P, 2, W], U8, name="xa_s", align_bytes=64)
+        wm_raw = keep.tile([P, W], I32, name="wm_raw", align_bytes=64)
+        wm_w = keep.tile([P, W], I32, name="wm_w", align_bytes=64)
+        wm_sraw = keep.tile([P, 1, W], U8, name="wm_sraw", align_bytes=64)
+        wm_s = keep.tile([P, W], U8, name="wm_s", align_bytes=64)
+        warm_in = keep.tile([P, 8], F32, name="warm_in")
+        warm_out = keep.tile([P, 8], F32, name="warm_out")
+
+        for plane in (wa_sraw, xa_s, wm_sraw):
+            nc.vector.memset(plane[:].bitcast(I32), 0)
+        nc.vector.memset(warm_in[:], 0.0)
+
+        queues = (nc.sync, nc.scalar)
+        for row in range(4):
+            load_scale_rows_spread(queues[row % 2], wb_sraw, wb_scales, row)
+        for quad in range(2):
+            load_scale_rows(queues[quad], wa_sraw, wa_scales, quad)
+        nc.sync.dma_start(out=wb_raw[:].bitcast(I32), in_=wb_words[0].bitcast(I32))
+        nc.scalar.dma_start(out=xb_w[:], in_=xb_words[0].rearrange("p n t -> p (n t)").bitcast(I32))
+        for row in range(4):
+            load_scale_rows_spread(queues[row % 2], xb_s, xb_scales, row)
+        nc.scalar.activation(warm_out[:], warm_in[:], RELU)
+        nc.sync.dma_start(out=wa_raw[:], in_=wa_words.rearrange("g p n t -> p g (n t)").bitcast(I32))
+        for quad in range(2, QUADS):
+            load_scale_rows(nc.sync, wa_sraw, wa_scales, quad)
+        nc.sync.dma_start(idx_b[:], offs2)
+        nc.sync.dma_start(out=xa_w[:].bitcast(I32), in_=xa_words.rearrange("g p c -> p g c").bitcast(I32))
+        for quad in range(3):
+            load_scale_rows(nc.sync, xa_s, xa_scales, quad)
+        nc.sync.dma_start(idx_a[:], offs)
+        load_scale_rows(nc.sync, xa_s, xa_scales, 3)
+        nc.sync.dma_start(out=wm_raw[:], in_=wm_words[0].rearrange("p n t -> p (n t)").bitcast(I32))
+        for quad in range(QUADS):
+            load_scale_rows(nc.sync, wm_sraw, wm_scales, quad)
+
+        deal(nc.vector, wb_w[:].bitcast(U16).unsqueeze(1), wb_raw[:].bitcast(U16).unsqueeze(1))
+        deal(nc.vector, wb_s[:].unsqueeze(1), wb_sraw[:])
+
+        zb = []
+        banks = list(range(8))
+        for r in range(PACK):
+            table = keep.tile([P, W], F32, name=f"zb{r}")
+            width = HALF if r == 0 else W
+            for c0 in range(0, W, width):
+                acc = psum.tile([P, width], F32, name=f"zb_acc{r}_{c0}", tag=f"bank{banks.pop(0)}")
+                nc.tensor.matmul_mx(
+                    out=acc[:],
+                    lhsT=wb_w[:, 2 * P * r : 2 * P * (r + 1)].bitcast(FP4X4),
+                    lhsT_scale=wb_s[:, P * r : P * (r + 1)],
+                    rhs=xb_w[:, c0 : c0 + width].bitcast(FP8X4),
+                    rhs_scale=xb_s[:, 0, c0 : c0 + width],
+                    start=True,
+                    stop=True,
+                )
+                nc.scalar.copy(table[:, c0 : c0 + width], acc[:])
+            zb.append(table)
+
+        deal(nc.vector, wa_s[:], wa_sraw[:])
+        deal(nc.vector, wa_w[:], wa_raw[:])
+
+        za = []
+        for r in range(PACK):
+            acc = psum.tile([P, W], F32, name=f"za_acc{r}", tag=f"bank{(PACK + 1 + r) % 8}")
+            for g in range(2):
+                nc.tensor.matmul_mx(
+                    out=acc[:],
+                    lhsT=wa_w[:, g, P * r : P * (r + 1)].bitcast(FP8X4),
+                    lhsT_scale=wa_s[:, g, P * r : P * (r + 1)],
+                    rhs=xa_w[:, g, :].bitcast(FP4X4),
+                    rhs_scale=xa_s[:, g, :],
+                    start=(g == 0),
+                    stop=(g == 1),
+                )
+            table = keep.tile([P, W], F32, name=f"za{r}")
+            nc.scalar.copy(table[:], acc[:])
+            za.append(table)
+
+        deal(nc.gpsimd, wm_w[:].unsqueeze(1), wm_raw[:].unsqueeze(1))
+        deal(nc.gpsimd, wm_s[:].unsqueeze(1), wm_sraw[:])
+
+        y_w = keep.tile([P, W], U32, name="y_w", align_bytes=64)
+        y_s = keep.tile([P, W], U8, name="y_s", align_bytes=64)
+        out_rows = out_0.rearrange("(p r) t -> p r t", r=PACK)
+        out_words = out_1[0].rearrange("p t r -> p (t r)").bitcast(I32)
+
+        def listed(idx, t0, n):
+            return idx[:, t0 // LIST_ROWS : (t0 + n) // LIST_ROWS]
+
+        def gather_b(t0, n, tags):
+            picked = []
+            for rows, tag in zip(((0,), (1, 2, 3)), tags):
+                tile = keep.tile([P, len(rows), n], F32, name=f"picked{t0}_{rows[0]}", tag=tag, align_bytes=64)
+                for k, r in enumerate(rows):
+                    nc.vector.tensor_copy(tile[:, k, :], zb[r][:].indirect(listed(idx_b, t0, n)))
+                    picked.append(tile[:, k, :])
+            return picked
+
+        def gather_a(t0, n, picked, tag):
+            summed = keep.tile([P, PACK, n], F32, name=f"summed{t0}", tag=tag, align_bytes=64)
+            for r in range(PACK):
+                nc.vector.tensor_tensor(summed[:, r, :], za[r][:].indirect(listed(idx_a, t0, n)), picked[r], ADD)
+            return summed
+
+        def relu_round(c, summed, on_vector=False):
+            h_bf = keep.tile([P, STEP, PACK], BF16, name=f"h_bf{c}", tag=f"h_bf{c}", align_bytes=64)
+            if on_vector:
+                nc.vector.tensor_scalar_max(h_bf[:], summed.rearrange("p r t -> p t r"), 0.0)
+            else:
+                nc.scalar.activation(h_bf[:], summed.rearrange("p r t -> p t r"), RELU)
+            return h_bf
+
+        def next_layer(c, h_bf, on_vector=False):
+            t0 = c * STEP
+            h_w = keep.tile([P, STEP], U32, name=f"h_w{c}", align_bytes=64)
+            h_s = keep.tile([P, STEP], U8, name=f"h_s{c}", align_bytes=64)
+            nc.vector.quantize_mx(out=h_w[:].bitcast(FP8X4), scales=h_s[:], in_=h_bf[:].rearrange("p t r -> p (t r)"))
+            acc = psum.tile([P, PACK, STEP], F32, name=f"y_acc{c}", tag=f"bank{c + 1}")
+            for r in range(PACK):
+                nc.tensor.matmul_mx(
+                    out=acc[:, r, :],
+                    lhsT=wm_w[:, P * r : P * (r + 1)].bitcast(FP8X4),
+                    lhsT_scale=wm_s[:, P * r : P * (r + 1)],
+                    rhs=h_w[:].bitcast(FP8X4),
+                    rhs_scale=h_s[:],
+                    start=True,
+                    stop=True,
+                )
+            y_bf = keep.tile([P, STEP, PACK], BF16, name=f"y_bf{c}", align_bytes=64)
+            y = keep.tile([P, PACK, STEP], F32, name=f"y{c}")
+            nc.scalar.copy(y[:], acc[:])
+            nc.sync.dma_start(out=out_rows[:, :, t0 : t0 + STEP], in_=y[:])
+            if on_vector:
+                nc.vector.tensor_copy(y_bf[:], y[:].rearrange("p r t -> p t r"))
+            else:
+                nc.scalar.copy(y_bf[:], acc[:].rearrange("p r t -> p t r"))
+            return y_bf
+
+        def planes(c, y_bf):
+            t0 = c * STEP
+            nc.vector.quantize_mx(
+                out=y_w[:, t0 : t0 + STEP].bitcast(FP8X4),
+                scales=y_s[:, t0 : t0 + STEP],
+                in_=y_bf[:].rearrange("p t r -> p (t r)"),
+            )
+            nc.sync.dma_start(out=out_words[:, t0 : t0 + STEP], in_=y_w[:, t0 : t0 + STEP].bitcast(I32))
+
+        picked = gather_b(0, HALF, ("picked_early", "picked_late"))
+        summed = gather_a(0, HALF, picked, "summed_early")
+        h0 = relu_round(0, summed[:, :, 0:STEP])
+        h1 = relu_round(1, summed[:, :, STEP:HALF])
+        picked = gather_b(2 * STEP, STEP, ("picked_late", "picked_early"))
+        y0 = next_layer(0, h0)
+        summed = gather_a(2 * STEP, STEP, picked, "h_bf0")
+        y1 = next_layer(1, h1)
+        h2 = relu_round(2, summed[:])
+        picked = gather_b(3 * STEP, STEP, ("h_bf1", "picked_late"))
+        planes(0, y0)
+        y2 = next_layer(2, h2)
+        summed = gather_a(3 * STEP, STEP, picked, "h_bf2")
+        h3 = relu_round(3, summed[:], on_vector=True)
+        planes(1, y1)
+        y3 = next_layer(3, h3, on_vector=True)
+        planes(2, y2)
+        planes(3, y3)
+        for quad in range(QUADS):
+            (nc.sync if quad % 2 == 0 else nc.scalar).dma_start(
+                out=out_2[0, 4 * quad : 4 * quad + 4, :].bitcast(I32),
+                in_=y_s[32 * quad : 32 * quad + 4, :].bitcast(I32),
+            )

@@ -38,10 +38,10 @@ def load_scale_rows_spread(queue, plane, scales, row):
     )
 
 
-def deal(engine, dealt, raw):
+def deal(engine, dealt, raw, run):
     engine.tensor_copy(
-        out=dealt.rearrange("p g (r m) -> p g r m", r=PACK),
-        in_=raw.rearrange("p g (m r) -> p g r m", r=PACK),
+        out=dealt.rearrange("p g (r c i) -> p g c r i", r=PACK, i=run),
+        in_=raw.rearrange("p g (c i r) -> p g c r i", r=PACK, i=run),
     )
 
 
@@ -53,6 +53,7 @@ def tile_moe_combined_hidden_next_layer_pl_kernel(
     with ExitStack() as ctx:
         lists = ctx.enter_context(tc.tile_pool(name="lists", bufs=1))
         keep = ctx.enter_context(tc.tile_pool(name="keep", bufs=1))
+        shared = ctx.enter_context(tc.tile_pool(name="shared", bufs=1))
         psum = ctx.enter_context(tc.psum_pool(name="psum", bufs=1))
 
         idx_a = lists.tile([P, W // LIST_ROWS], U16, name="idx_a")
@@ -64,9 +65,9 @@ def tile_moe_combined_hidden_next_layer_pl_kernel(
         wb_s = keep.tile([P, W], U8, name="wb_s", align_bytes=64)
         xb_w = keep.tile([P, W], I32, name="xb_w", align_bytes=64)
         xb_s = keep.tile([P, 1, W], U8, name="xb_s", align_bytes=64)
-        wa_raw = keep.tile([P, 2, W], I32, name="wa_raw", tag="picked_late", align_bytes=64)
+        wa_raw = keep.tile([P, 2, W], I32, name="wa_raw", align_bytes=64)
         wa_w = keep.tile([P, 2, W], I32, name="wa_w", align_bytes=64)
-        wa_sraw = keep.tile([P, 2, W], U8, name="wa_sraw", tag="picked_early", align_bytes=64)
+        wa_sraw = shared.tile([P, 2, W], U8, name="wa_sraw", offset=1792)
         wa_s = keep.tile([P, 2, W], U8, name="wa_s", align_bytes=64)
         xa_w = keep.tile([P, 2, 2 * W], U8, name="xa_w", align_bytes=64)
         xa_s = keep.tile([P, 2, W], U8, name="xa_s", align_bytes=64)
@@ -84,28 +85,29 @@ def tile_moe_combined_hidden_next_layer_pl_kernel(
         queues = (nc.sync, nc.scalar)
         for row in range(4):
             load_scale_rows_spread(queues[row % 2], wb_sraw, wb_scales, row)
-        for quad in range(2):
-            load_scale_rows(queues[quad], wa_sraw, wa_scales, quad)
+        for row in range(2):
+            load_scale_rows_spread(queues[row], xb_s, xb_scales, row)
         nc.sync.dma_start(out=wb_raw[:].bitcast(I32), in_=wb_words[0].bitcast(I32))
         nc.scalar.dma_start(out=xb_w[:], in_=xb_words[0].rearrange("p n t -> p (n t)").bitcast(I32))
-        for row in range(4):
+        for row in range(2, 4):
             load_scale_rows_spread(queues[row % 2], xb_s, xb_scales, row)
         nc.scalar.activation(warm_out[:], warm_in[:], RELU)
+        nc.sync.dma_start(idx_b[:], offs2)
+        for quad in range(2):
+            load_scale_rows(nc.gpsimd, wa_sraw, wa_scales, quad)
         nc.sync.dma_start(out=wa_raw[:], in_=wa_words.rearrange("g p n t -> p g (n t)").bitcast(I32))
         for quad in range(2, QUADS):
             load_scale_rows(nc.sync, wa_sraw, wa_scales, quad)
-        nc.sync.dma_start(idx_b[:], offs2)
-        nc.sync.dma_start(out=xa_w[:].bitcast(I32), in_=xa_words.rearrange("g p c -> p g c").bitcast(I32))
-        for quad in range(3):
+        for quad in range(QUADS):
             load_scale_rows(nc.sync, xa_s, xa_scales, quad)
+        nc.sync.dma_start(out=xa_w[:].bitcast(I32), in_=xa_words.rearrange("g p c -> p g c").bitcast(I32))
         nc.sync.dma_start(idx_a[:], offs)
-        load_scale_rows(nc.sync, xa_s, xa_scales, 3)
         nc.sync.dma_start(out=wm_raw[:], in_=wm_words[0].rearrange("p n t -> p (n t)").bitcast(I32))
         for quad in range(QUADS):
             load_scale_rows(nc.sync, wm_sraw, wm_scales, quad)
 
-        deal(nc.vector, wb_w[:].bitcast(U16).unsqueeze(1), wb_raw[:].bitcast(U16).unsqueeze(1))
-        deal(nc.vector, wb_s[:].unsqueeze(1), wb_sraw[:])
+        deal(nc.vector, wb_w[:].bitcast(U16).unsqueeze(1), wb_raw[:].bitcast(U16).unsqueeze(1), 8)
+        deal(nc.vector, wb_s[:].unsqueeze(1), wb_sraw[:], 16)
 
         zb = []
         banks = list(range(8))
@@ -126,8 +128,8 @@ def tile_moe_combined_hidden_next_layer_pl_kernel(
                 nc.scalar.copy(table[:, c0 : c0 + width], acc[:])
             zb.append(table)
 
-        deal(nc.vector, wa_s[:], wa_sraw[:])
-        deal(nc.vector, wa_w[:], wa_raw[:])
+        deal(nc.vector, wa_w[:], wa_raw[:], 4)
+        deal(nc.vector, wa_s[:], wa_sraw[:], 16)
 
         za = []
         for r in range(PACK):
@@ -146,8 +148,8 @@ def tile_moe_combined_hidden_next_layer_pl_kernel(
             nc.scalar.copy(table[:], acc[:])
             za.append(table)
 
-        deal(nc.gpsimd, wm_w[:].unsqueeze(1), wm_raw[:].unsqueeze(1))
-        deal(nc.gpsimd, wm_s[:].unsqueeze(1), wm_sraw[:])
+        deal(nc.vector, wm_w[:].unsqueeze(1), wm_raw[:].unsqueeze(1), 4)
+        deal(nc.vector, wm_s[:].unsqueeze(1), wm_sraw[:], 16)
 
         y_w = keep.tile([P, W], U32, name="y_w", align_bytes=64)
         y_s = keep.tile([P, W], U8, name="y_s", align_bytes=64)
@@ -157,35 +159,29 @@ def tile_moe_combined_hidden_next_layer_pl_kernel(
         def listed(idx, t0, n):
             return idx[:, t0 // LIST_ROWS : (t0 + n) // LIST_ROWS]
 
-        def gather_b(t0, n, tags):
-            picked = []
-            for rows, tag in zip(((0,), (1, 2, 3)), tags):
-                tile = keep.tile([P, len(rows), n], F32, name=f"picked{t0}_{rows[0]}", tag=tag, align_bytes=64)
-                for k, r in enumerate(rows):
-                    nc.vector.tensor_copy(tile[:, k, :], zb[r][:].indirect(listed(idx_b, t0, n)))
-                    picked.append(tile[:, k, :])
-            return picked
+        def gather_b(t0, n, rows, picked):
+            for k, r in enumerate(rows):
+                nc.vector.tensor_copy(picked[:, k, :], zb[r][:].indirect(listed(idx_b, t0, n)))
 
-        def gather_a(t0, n, picked, tag):
-            summed = keep.tile([P, PACK, n], F32, name=f"summed{t0}", tag=tag, align_bytes=64)
+        def gather_a(t0, n, picked, summed):
             for r in range(PACK):
                 nc.vector.tensor_tensor(summed[:, r, :], za[r][:].indirect(listed(idx_a, t0, n)), picked[r], ADD)
-            return summed
 
-        def relu_round(c, summed, on_vector=False):
-            h_bf = keep.tile([P, STEP, PACK], BF16, name=f"h_bf{c}", tag=f"h_bf{c}", align_bytes=64)
+        def relu_round(t0, n, summed, on_vector=False):
+            h_bf = keep.tile([P, n, PACK], BF16, name=f"h_bf{t0}", tag=f"h_bf{t0}", align_bytes=64)
             if on_vector:
                 nc.vector.tensor_scalar_max(h_bf[:], summed.rearrange("p r t -> p t r"), 0.0)
             else:
                 nc.scalar.activation(h_bf[:], summed.rearrange("p r t -> p t r"), RELU)
             return h_bf
 
-        def next_layer(c, h_bf, on_vector=False):
-            t0 = c * STEP
-            h_w = keep.tile([P, STEP], U32, name=f"h_w{c}", align_bytes=64)
-            h_s = keep.tile([P, STEP], U8, name=f"h_s{c}", align_bytes=64)
+        y_banks = [1, 2, 3, 4, 5]
+
+        def next_layer(t0, n, h_bf, y, y_bf, on_vector=False):
+            h_w = keep.tile([P, n], U32, name=f"h_w{t0}", align_bytes=64)
+            h_s = keep.tile([P, n], U8, name=f"h_s{t0}", align_bytes=64)
             nc.vector.quantize_mx(out=h_w[:].bitcast(FP8X4), scales=h_s[:], in_=h_bf[:].rearrange("p t r -> p (t r)"))
-            acc = psum.tile([P, PACK, STEP], F32, name=f"y_acc{c}", tag=f"bank{c + 1}")
+            acc = psum.tile([P, PACK, n], F32, name=f"y_acc{t0}", tag=f"bank{y_banks.pop(0)}")
             for r in range(PACK):
                 nc.tensor.matmul_mx(
                     out=acc[:, r, :],
@@ -196,43 +192,72 @@ def tile_moe_combined_hidden_next_layer_pl_kernel(
                     start=True,
                     stop=True,
                 )
-            y_bf = keep.tile([P, STEP, PACK], BF16, name=f"y_bf{c}", align_bytes=64)
-            y = keep.tile([P, PACK, STEP], F32, name=f"y{c}")
-            nc.scalar.copy(y[:], acc[:])
-            nc.sync.dma_start(out=out_rows[:, :, t0 : t0 + STEP], in_=y[:])
             if on_vector:
-                nc.vector.tensor_copy(y_bf[:], y[:].rearrange("p r t -> p t r"))
-            else:
-                nc.scalar.copy(y_bf[:], acc[:].rearrange("p r t -> p t r"))
-            return y_bf
+                nc.vector.tensor_copy(y_bf, acc[:].rearrange("p r t -> p t r"))
+            nc.scalar.copy(y, acc[:])
+            if not on_vector:
+                nc.scalar.copy(y_bf, acc[:].rearrange("p r t -> p t r"))
 
-        def planes(c, y_bf):
-            t0 = c * STEP
+        def store_y(t0, y):
+            nc.sync.dma_start(out=out_rows[:, :, t0 : t0 + STEP], in_=y[:])
+
+        def planes(t0, n, y_bf):
             nc.vector.quantize_mx(
-                out=y_w[:, t0 : t0 + STEP].bitcast(FP8X4),
-                scales=y_s[:, t0 : t0 + STEP],
+                out=y_w[:, t0 : t0 + n].bitcast(FP8X4),
+                scales=y_s[:, t0 : t0 + n],
                 in_=y_bf[:].rearrange("p t r -> p (t r)"),
             )
-            nc.sync.dma_start(out=out_words[:, t0 : t0 + STEP], in_=y_w[:, t0 : t0 + STEP].bitcast(I32))
 
-        picked = gather_b(0, HALF, ("picked_early", "picked_late"))
-        summed = gather_a(0, HALF, picked, "summed_early")
-        h0 = relu_round(0, summed[:, :, 0:STEP])
-        h1 = relu_round(1, summed[:, :, STEP:HALF])
-        picked = gather_b(2 * STEP, STEP, ("picked_late", "picked_early"))
-        y0 = next_layer(0, h0)
-        summed = gather_a(2 * STEP, STEP, picked, "h_bf0")
-        y1 = next_layer(1, h1)
-        h2 = relu_round(2, summed[:])
-        picked = gather_b(3 * STEP, STEP, ("h_bf1", "picked_late"))
-        planes(0, y0)
-        y2 = next_layer(2, h2)
-        summed = gather_a(3 * STEP, STEP, picked, "h_bf2")
-        h3 = relu_round(3, summed[:], on_vector=True)
-        planes(1, y1)
-        y3 = next_layer(3, h3, on_vector=True)
-        planes(2, y2)
-        planes(3, y3)
+        def store_words(t0, n):
+            nc.sync.dma_start(out=out_words[:, t0 : t0 + n], in_=y_w[:, t0 : t0 + n].bitcast(I32))
+
+        def summed_tile(t0, n, after):
+            return keep.tile([P, PACK, n], F32, name=f"summed{t0}", tag=after, align_bytes=64)
+
+        y = [keep.tile([P, PACK, STEP], F32, name=f"y{c}") for c in range(4)]
+        y_bf01 = keep.tile([P, HALF, PACK], BF16, name="y_bf01", align_bytes=64)
+        y_bf2 = keep.tile([P, STEP, PACK], BF16, name="y_bf2", align_bytes=64)
+        y_bf3 = keep.tile([P, STEP, PACK], BF16, name="y_bf3", align_bytes=64)
+
+        first = shared.tile([P, 3, HALF], F32, name="picked_first", offset=2560)
+        rest0 = shared.tile([P, 1, STEP], F32, name="picked_rest0", offset=1536)
+        rest1 = shared.tile([P, 1, STEP], F32, name="picked_rest1", offset=2048)
+        gather_b(0, HALF, (0, 1, 2), first)
+        gather_b(0, STEP, (3,), rest0)
+        gather_b(STEP, STEP, (3,), rest1)
+
+        s0 = summed_tile(0, STEP, "summed0")
+        gather_a(0, STEP, [first[:, k, 0:STEP] for k in range(3)] + [rest0[:, 0, :]], s0[:])
+        h0 = relu_round(0, STEP, s0[:])
+        s1 = shared.tile([P, PACK, STEP], F32, name="summed128", offset=0)
+        gather_a(128, STEP, [first[:, k, STEP:HALF] for k in range(3)] + [rest1[:, 0, :]], s1[:])
+        h1 = relu_round(128, STEP, s1[:])
+        next_layer(0, STEP, h0, y[0][:], y_bf01[:, 0:STEP, :])
+        store_y(0, y[0])
+        third = keep.tile([P, PACK, STEP], F32, name="picked_third", tag="h_bf0", align_bytes=64)
+        gather_b(HALF, STEP, range(PACK), third)
+        next_layer(128, STEP, h1, y[1][:], y_bf01[:, STEP:HALF, :])
+        store_y(128, y[1])
+        s2 = summed_tile(256, STEP, "h_bf128")
+        gather_a(256, STEP, [third[:, r, :] for r in range(PACK)], s2[:])
+        h2 = relu_round(256, STEP, s2[:])
+        last = keep.tile([P, PACK, STEP], F32, name="picked_last", tag="h_bf0", align_bytes=64)
+        gather_b(384, STEP, range(PACK), last)
+        next_layer(256, STEP, h2, y[2][:], y_bf2[:])
+        store_y(256, y[2])
+        planes(0, HALF, y_bf01)
+        store_words(0, HALF)
+        s3 = summed_tile(384, STEP, "h_bf256")
+        gather_a(384, 64, [last[:, r, 0:64] for r in range(PACK)], s3[:, :, 0:64])
+        h3 = relu_round(384, 64, s3[:, :, 0:64], on_vector=True)
+        next_layer(384, 64, h3, y[3][:, :, 0:64], y_bf3[:, 0:64, :], on_vector=True)
+        gather_a(448, 64, [last[:, r, 64:STEP] for r in range(PACK)], s3[:, :, 64:STEP])
+        h4 = relu_round(448, 64, s3[:, :, 64:STEP], on_vector=True)
+        next_layer(448, 64, h4, y[3][:, :, 64:STEP], y_bf3[:, 64:STEP, :], on_vector=True)
+        store_y(384, y[3])
+        planes(256, STEP, y_bf2)
+        planes(384, STEP, y_bf3)
+        store_words(HALF, HALF)
         for quad in range(QUADS):
             (nc.sync if quad % 2 == 0 else nc.scalar).dma_start(
                 out=out_2[0, 4 * quad : 4 * quad + 4, :].bitcast(I32),

@@ -65,9 +65,9 @@ def tile_moe_combined_hidden_next_layer_pl_kernel(
         wb_s = keep.tile([P, W], U8, name="wb_s", align_bytes=64)
         xb_w = keep.tile([P, W], I32, name="xb_w", align_bytes=64)
         xb_s = keep.tile([P, 1, W], U8, name="xb_s", align_bytes=64)
-        wa_raw = keep.tile([P, 2, W], I32, name="wa_raw", align_bytes=64)
+        wa_raw = shared.tile([P, 2, W], I32, name="wa_raw", offset=0)
         wa_w = keep.tile([P, 2, W], I32, name="wa_w", align_bytes=64)
-        wa_sraw = shared.tile([P, 2, W], U8, name="wa_sraw", offset=1792)
+        wa_sraw = keep.tile([P, 2, W], U8, name="wa_sraw", tag="picked_early", align_bytes=64)
         wa_s = keep.tile([P, 2, W], U8, name="wa_s", align_bytes=64)
         xa_w = keep.tile([P, 2, 2 * W], U8, name="xa_w", align_bytes=64)
         xa_s = keep.tile([P, 2, W], U8, name="xa_s", align_bytes=64)
@@ -93,11 +93,9 @@ def tile_moe_combined_hidden_next_layer_pl_kernel(
             load_scale_rows_spread(queues[row % 2], xb_s, xb_scales, row)
         nc.scalar.activation(warm_out[:], warm_in[:], RELU)
         nc.sync.dma_start(idx_b[:], offs2)
-        for quad in range(2):
-            load_scale_rows(nc.gpsimd, wa_sraw, wa_scales, quad)
-        nc.sync.dma_start(out=wa_raw[:], in_=wa_words.rearrange("g p n t -> p g (n t)").bitcast(I32))
-        for quad in range(2, QUADS):
+        for quad in range(QUADS):
             load_scale_rows(nc.sync, wa_sraw, wa_scales, quad)
+        nc.sync.dma_start(out=wa_raw[:], in_=wa_words.rearrange("g p n t -> p g (n t)").bitcast(I32))
         for quad in range(QUADS):
             load_scale_rows(nc.sync, xa_s, xa_scales, quad)
         nc.sync.dma_start(out=xa_w[:].bitcast(I32), in_=xa_words.rearrange("g p c -> p g c").bitcast(I32))
@@ -128,8 +126,8 @@ def tile_moe_combined_hidden_next_layer_pl_kernel(
                 nc.scalar.copy(table[:, c0 : c0 + width], acc[:])
             zb.append(table)
 
-        deal(nc.vector, wa_w[:], wa_raw[:], 4)
         deal(nc.vector, wa_s[:], wa_sraw[:], 16)
+        deal(nc.vector, wa_w[:], wa_raw[:], 4)
 
         za = []
         for r in range(PACK):
@@ -148,8 +146,8 @@ def tile_moe_combined_hidden_next_layer_pl_kernel(
             nc.scalar.copy(table[:], acc[:])
             za.append(table)
 
-        deal(nc.vector, wm_w[:].unsqueeze(1), wm_raw[:].unsqueeze(1), 4)
-        deal(nc.vector, wm_s[:].unsqueeze(1), wm_sraw[:], 16)
+        deal(nc.gpsimd, wm_w[:].unsqueeze(1), wm_raw[:].unsqueeze(1), 4)
+        deal(nc.gpsimd, wm_s[:].unsqueeze(1), wm_sraw[:], 16)
 
         y_w = keep.tile([P, W], U32, name="y_w", align_bytes=64)
         y_s = keep.tile([P, W], U8, name="y_s", align_bytes=64)
@@ -198,8 +196,8 @@ def tile_moe_combined_hidden_next_layer_pl_kernel(
             if not on_vector:
                 nc.scalar.copy(y_bf, acc[:].rearrange("p r t -> p t r"))
 
-        def store_y(t0, y):
-            nc.sync.dma_start(out=out_rows[:, :, t0 : t0 + STEP], in_=y[:])
+        def store_y(t0, y, queue=nc.sync):
+            queue.dma_start(out=out_rows[:, :, t0 : t0 + STEP], in_=y[:])
 
         def planes(t0, n, y_bf):
             nc.vector.quantize_mx(
@@ -219,47 +217,57 @@ def tile_moe_combined_hidden_next_layer_pl_kernel(
         y_bf2 = keep.tile([P, STEP, PACK], BF16, name="y_bf2", align_bytes=64)
         y_bf3 = keep.tile([P, STEP, PACK], BF16, name="y_bf3", align_bytes=64)
 
-        first = shared.tile([P, 3, HALF], F32, name="picked_first", offset=2560)
+        first = keep.tile([P, 1, HALF], F32, name="picked_first", tag="picked_early", align_bytes=64)
         rest0 = shared.tile([P, 1, STEP], F32, name="picked_rest0", offset=1536)
-        rest1 = shared.tile([P, 1, STEP], F32, name="picked_rest1", offset=2048)
-        gather_b(0, HALF, (0, 1, 2), first)
+        rest1 = shared.tile([P, 1, 3 * STEP], F32, name="picked_rest1", offset=2048)
+        middle = shared.tile([P, 5, HALF], F32, name="picked_middle", offset=3584)
+        gather_b(0, HALF, (0,), first)
+        gather_b(HALF, HALF, (0,), middle[:, 0:1, :])
+        for r in (1, 2):
+            for half in range(2):
+                gather_b(half * HALF, HALF, (r,), middle[:, 2 * r - 1 + half : 2 * r + half, :])
         gather_b(0, STEP, (3,), rest0)
-        gather_b(STEP, STEP, (3,), rest1)
+        gather_b(STEP, 3 * STEP, (3,), rest1)
+
+        def picked(t0, n):
+            half, off = divmod(t0, HALF)
+            cols = slice(off, off + n)
+            head = first[:, 0, cols] if half == 0 else middle[:, 0, cols]
+            tail = rest0[:, 0, :] if t0 == 0 else rest1[:, 0, t0 - STEP : t0 - STEP + n]
+            return [head, middle[:, 1 + half, cols], middle[:, 3 + half, cols], tail]
 
         s0 = summed_tile(0, STEP, "summed0")
-        gather_a(0, STEP, [first[:, k, 0:STEP] for k in range(3)] + [rest0[:, 0, :]], s0[:])
+        gather_a(0, STEP, picked(0, STEP), s0[:])
         h0 = relu_round(0, STEP, s0[:])
         s1 = shared.tile([P, PACK, STEP], F32, name="summed128", offset=0)
-        gather_a(128, STEP, [first[:, k, STEP:HALF] for k in range(3)] + [rest1[:, 0, :]], s1[:])
+        gather_a(128, STEP, picked(128, STEP), s1[:])
         h1 = relu_round(128, STEP, s1[:])
         next_layer(0, STEP, h0, y[0][:], y_bf01[:, 0:STEP, :])
         store_y(0, y[0])
-        third = keep.tile([P, PACK, STEP], F32, name="picked_third", tag="h_bf0", align_bytes=64)
-        gather_b(HALF, STEP, range(PACK), third)
+        s2 = summed_tile(256, STEP, "h_bf0")
+        gather_a(256, STEP, picked(256, STEP), s2[:])
+        h2 = relu_round(256, STEP, s2[:])
         next_layer(128, STEP, h1, y[1][:], y_bf01[:, STEP:HALF, :])
         store_y(128, y[1])
-        s2 = summed_tile(256, STEP, "h_bf128")
-        gather_a(256, STEP, [third[:, r, :] for r in range(PACK)], s2[:])
-        h2 = relu_round(256, STEP, s2[:])
-        last = keep.tile([P, PACK, STEP], F32, name="picked_last", tag="h_bf0", align_bytes=64)
-        gather_b(384, STEP, range(PACK), last)
+        s3 = summed_tile(384, 64, "h_bf128")
+        gather_a(384, 64, picked(384, 64), s3[:])
         next_layer(256, STEP, h2, y[2][:], y_bf2[:])
         store_y(256, y[2])
+        h3 = relu_round(384, 64, s3[:], on_vector=True)
+        next_layer(384, 64, h3, y[3][:, :, 0:64], y_bf3[:, 0:64, :], on_vector=True)
+        s4 = summed_tile(448, 64, "h_bf256")
+        gather_a(448, 64, picked(448, 64), s4[:])
+        h4 = relu_round(448, 64, s4[:], on_vector=True)
+        next_layer(448, 64, h4, y[3][:, :, 64:STEP], y_bf3[:, 64:STEP, :], on_vector=True)
         planes(0, HALF, y_bf01)
         store_words(0, HALF)
-        s3 = summed_tile(384, STEP, "h_bf256")
-        gather_a(384, 64, [last[:, r, 0:64] for r in range(PACK)], s3[:, :, 0:64])
-        h3 = relu_round(384, 64, s3[:, :, 0:64], on_vector=True)
-        next_layer(384, 64, h3, y[3][:, :, 0:64], y_bf3[:, 0:64, :], on_vector=True)
-        gather_a(448, 64, [last[:, r, 64:STEP] for r in range(PACK)], s3[:, :, 64:STEP])
-        h4 = relu_round(448, 64, s3[:, :, 64:STEP], on_vector=True)
-        next_layer(448, 64, h4, y[3][:, :, 64:STEP], y_bf3[:, 64:STEP, :], on_vector=True)
-        store_y(384, y[3])
+        store_y(384, y[3], nc.scalar)
         planes(256, STEP, y_bf2)
+        store_words(HALF, STEP)
         planes(384, STEP, y_bf3)
-        store_words(HALF, HALF)
+        store_words(384, STEP)
         for quad in range(QUADS):
-            (nc.sync if quad % 2 == 0 else nc.scalar).dma_start(
+            (nc.sync if quad < 2 else nc.scalar).dma_start(
                 out=out_2[0, 4 * quad : 4 * quad + 4, :].bitcast(I32),
                 in_=y_s[32 * quad : 32 * quad + 4, :].bitcast(I32),
             )

@@ -15,34 +15,50 @@ ADD = mybir.AluOpType.add
 
 P = 128
 PACK = 4
-W = 512
+WIDTH = 512
+PASSES_A = 2
 QUADS = 4
+QUAD = P // QUADS
+ROWS = 4
 LIST_ROWS = 16
-HALF = 256
-STEP = 128
+LINE = 16
+BANKS = 8
+CHUNK = 128
+HALF = 2 * CHUNK
+PIECE = CHUNK // 2
+EARLY = 3 * CHUNK
+CHUNK_BYTES = 4 * CHUNK
 
-FLOPS = 2 * (1024 * 512 * 512 + 512 * 512 * 512 + 512 * 512 * 512)
+FLOPS = 2 * WIDTH * WIDTH * (PASSES_A * WIDTH + WIDTH + WIDTH)
 
 
 def load_scale_rows(queue, plane, scales, quad):
     queue.dma_start(
-        out=plane[32 * quad : 32 * quad + 4].bitcast(I32),
-        in_=scales[:, 4 * quad : 4 * quad + 4, :].rearrange("g q c -> q g c").bitcast(I32),
+        out=plane[QUAD * quad : QUAD * quad + ROWS].bitcast(I32),
+        in_=scales[:, ROWS * quad : ROWS * (quad + 1), :].rearrange("g q c -> q g c").bitcast(I32),
     )
 
 
 def load_scale_rows_spread(queue, plane, scales, row):
     queue.dma_start(
-        out=plane[row:P:4, 0, :].bitcast(I32),
-        in_=scales[0, row:16:4, :].bitcast(I32).unsqueeze(1).to_broadcast([QUADS, 8, W // 4]),
+        out=plane[row:P:ROWS, 0, :].bitcast(I32),
+        in_=scales[0, row : QUADS * ROWS : ROWS, :]
+        .bitcast(I32)
+        .unsqueeze(1)
+        .to_broadcast([QUADS, QUAD // ROWS, WIDTH // 4]),
     )
 
 
-def deal(engine, dealt, raw, run):
+def deal(engine, dealt, raw, item_bytes):
+    run = LINE // item_bytes
     engine.tensor_copy(
         out=dealt.rearrange("p g (r c i) -> p g c r i", r=PACK, i=run),
         in_=raw.rearrange("p g (c i r) -> p g c r i", r=PACK, i=run),
     )
+
+
+def by_token(slices):
+    return slices.rearrange("p r t -> p t r")
 
 
 def tile_moe_combined_hidden_next_layer_pl_kernel(
@@ -56,42 +72,38 @@ def tile_moe_combined_hidden_next_layer_pl_kernel(
         shared = ctx.enter_context(tc.tile_pool(name="shared", bufs=1))
         psum = ctx.enter_context(tc.psum_pool(name="psum", bufs=1))
 
-        idx_a = lists.tile([P, W // LIST_ROWS], U16, name="idx_a")
-        idx_b = lists.tile([P, W // LIST_ROWS], U16, name="idx_b")
+        idx_a = lists.tile([P, WIDTH // LIST_ROWS], U16, name="idx_a")
+        idx_b = lists.tile([P, WIDTH // LIST_ROWS], U16, name="idx_b")
 
-        wb_raw = keep.tile([P, 2 * W], U8, name="wb_raw", align_bytes=64)
-        wb_w = keep.tile([P, 2 * W], U8, name="wb_w", align_bytes=64)
-        wb_sraw = keep.tile([P, 1, W], U8, name="wb_sraw", align_bytes=64)
-        wb_s = keep.tile([P, W], U8, name="wb_s", align_bytes=64)
-        xb_w = keep.tile([P, W], I32, name="xb_w", align_bytes=64)
-        xb_s = keep.tile([P, 1, W], U8, name="xb_s", align_bytes=64)
-        wa_raw = shared.tile([P, 2, W], I32, name="wa_raw", offset=0)
-        wa_w = keep.tile([P, 2, W], I32, name="wa_w", align_bytes=64)
-        wa_sraw = keep.tile([P, 2, W], U8, name="wa_sraw", tag="picked_early", align_bytes=64)
-        wa_s = keep.tile([P, 2, W], U8, name="wa_s", align_bytes=64)
-        xa_w = keep.tile([P, 2, 2 * W], U8, name="xa_w", align_bytes=64)
-        xa_s = keep.tile([P, 2, W], U8, name="xa_s", align_bytes=64)
-        wm_raw = keep.tile([P, W], I32, name="wm_raw", align_bytes=64)
-        wm_w = keep.tile([P, W], I32, name="wm_w", align_bytes=64)
-        wm_sraw = keep.tile([P, 1, W], U8, name="wm_sraw", align_bytes=64)
-        wm_s = keep.tile([P, W], U8, name="wm_s", align_bytes=64)
-        warm_in = keep.tile([P, 8], F32, name="warm_in")
-        warm_out = keep.tile([P, 8], F32, name="warm_out")
+        wb_raw = keep.tile([P, 2 * WIDTH], U8, name="wb_raw", align_bytes=64)
+        wb_w = keep.tile([P, 2 * WIDTH], U8, name="wb_w", align_bytes=64)
+        wb_sraw = keep.tile([P, 1, WIDTH], U8, name="wb_sraw", align_bytes=64)
+        wb_s = keep.tile([P, WIDTH], U8, name="wb_s", align_bytes=64)
+        xb_w = keep.tile([P, WIDTH], I32, name="xb_w", align_bytes=64)
+        xb_s = keep.tile([P, 1, WIDTH], U8, name="xb_s", align_bytes=64)
+        wa_raw = shared.tile([P, PASSES_A, WIDTH], I32, name="wa_raw", offset=2 * CHUNK_BYTES)
+        wa_w = keep.tile([P, PASSES_A, WIDTH], I32, name="wa_w", align_bytes=64)
+        wa_sraw = keep.tile([P, PASSES_A, WIDTH], U8, name="wa_sraw", tag="wa_sraw", align_bytes=64)
+        wa_s = keep.tile([P, PASSES_A, WIDTH], U8, name="wa_s", align_bytes=64)
+        xa_w = keep.tile([P, PASSES_A, 2 * WIDTH], U8, name="xa_w", align_bytes=64)
+        xa_s = keep.tile([P, PASSES_A, WIDTH], U8, name="xa_s", align_bytes=64)
+        wm_raw = keep.tile([P, WIDTH], I32, name="wm_raw", align_bytes=64)
+        wm_w = keep.tile([P, WIDTH], I32, name="wm_w", align_bytes=64)
+        wm_sraw = keep.tile([P, 1, WIDTH], U8, name="wm_sraw", align_bytes=64)
+        wm_s = keep.tile([P, WIDTH], U8, name="wm_s", align_bytes=64)
 
-        for plane in (wa_sraw, xa_s, wm_sraw):
+        for plane in (xb_s, wa_sraw, xa_s, wm_sraw):
             nc.vector.memset(plane[:].bitcast(I32), 0)
-        nc.vector.memset(warm_in[:], 0.0)
 
         queues = (nc.sync, nc.scalar)
-        for row in range(4):
+        for row in range(ROWS):
             load_scale_rows_spread(queues[row % 2], wb_sraw, wb_scales, row)
-        for row in range(2):
-            load_scale_rows_spread(queues[row], xb_s, xb_scales, row)
+        for quad in range(QUADS // 2):
+            load_scale_rows(queues[quad % 2], xb_s, xb_scales, quad)
         nc.sync.dma_start(out=wb_raw[:].bitcast(I32), in_=wb_words[0].bitcast(I32))
         nc.scalar.dma_start(out=xb_w[:], in_=xb_words[0].rearrange("p n t -> p (n t)").bitcast(I32))
-        for row in range(2, 4):
-            load_scale_rows_spread(queues[row % 2], xb_s, xb_scales, row)
-        nc.scalar.activation(warm_out[:], warm_in[:], RELU)
+        for quad in range(QUADS // 2, QUADS):
+            load_scale_rows(queues[quad % 2], xb_s, xb_scales, quad)
         nc.sync.dma_start(idx_b[:], offs2)
         for quad in range(QUADS):
             load_scale_rows(nc.sync, wa_sraw, wa_scales, quad)
@@ -104,16 +116,20 @@ def tile_moe_combined_hidden_next_layer_pl_kernel(
         for quad in range(QUADS):
             load_scale_rows(nc.sync, wm_sraw, wm_scales, quad)
 
-        deal(nc.vector, wb_w[:].bitcast(U16).unsqueeze(1), wb_raw[:].bitcast(U16).unsqueeze(1), 8)
-        deal(nc.vector, wb_s[:].unsqueeze(1), wb_sraw[:], 16)
+        bank_turn = list(range(2 * BANKS))
+
+        def psum_tile(shape, name):
+            return psum.tile(shape, F32, name=name, tag=f"bank{bank_turn.pop(0) % BANKS}")
+
+        deal(nc.vector, wb_w[:].bitcast(U16).unsqueeze(1), wb_raw[:].bitcast(U16).unsqueeze(1), 2)
+        deal(nc.vector, wb_s[:].unsqueeze(1), wb_sraw[:], 1)
 
         zb = []
-        banks = list(range(8))
         for r in range(PACK):
-            table = keep.tile([P, W], F32, name=f"zb{r}")
-            width = HALF if r == 0 else W
-            for c0 in range(0, W, width):
-                acc = psum.tile([P, width], F32, name=f"zb_acc{r}_{c0}", tag=f"bank{banks.pop(0)}")
+            table = keep.tile([P, WIDTH], F32, name=f"zb{r}")
+            width = HALF if r == 0 else WIDTH
+            for c0 in range(0, WIDTH, width):
+                acc = psum_tile([P, width], f"zb_acc{r}_{c0}")
                 nc.tensor.matmul_mx(
                     out=acc[:],
                     lhsT=wb_w[:, 2 * P * r : 2 * P * (r + 1)].bitcast(FP4X4),
@@ -126,13 +142,13 @@ def tile_moe_combined_hidden_next_layer_pl_kernel(
                 nc.scalar.copy(table[:, c0 : c0 + width], acc[:])
             zb.append(table)
 
-        deal(nc.vector, wa_s[:], wa_sraw[:], 16)
+        deal(nc.vector, wa_s[:], wa_sraw[:], 1)
         deal(nc.vector, wa_w[:], wa_raw[:], 4)
 
         za = []
         for r in range(PACK):
-            acc = psum.tile([P, W], F32, name=f"za_acc{r}", tag=f"bank{(PACK + 1 + r) % 8}")
-            for g in range(2):
+            acc = psum_tile([P, WIDTH], f"za_acc{r}")
+            for g in range(PASSES_A):
                 nc.tensor.matmul_mx(
                     out=acc[:],
                     lhsT=wa_w[:, g, P * r : P * (r + 1)].bitcast(FP8X4),
@@ -140,46 +156,42 @@ def tile_moe_combined_hidden_next_layer_pl_kernel(
                     rhs=xa_w[:, g, :].bitcast(FP4X4),
                     rhs_scale=xa_s[:, g, :],
                     start=(g == 0),
-                    stop=(g == 1),
+                    stop=(g == PASSES_A - 1),
                 )
-            table = keep.tile([P, W], F32, name=f"za{r}")
+            table = keep.tile([P, WIDTH], F32, name=f"za{r}")
             nc.scalar.copy(table[:], acc[:])
             za.append(table)
 
         deal(nc.gpsimd, wm_w[:].unsqueeze(1), wm_raw[:].unsqueeze(1), 4)
-        deal(nc.gpsimd, wm_s[:].unsqueeze(1), wm_sraw[:], 16)
+        deal(nc.gpsimd, wm_s[:].unsqueeze(1), wm_sraw[:], 1)
 
-        y_w = keep.tile([P, W], U32, name="y_w", align_bytes=64)
-        y_s = keep.tile([P, W], U8, name="y_s", align_bytes=64)
+        y_w = keep.tile([P, WIDTH], U32, name="y_w", align_bytes=64)
+        y_s = keep.tile([P, WIDTH], U8, name="y_s", align_bytes=64)
         out_rows = out_0.rearrange("(p r) t -> p r t", r=PACK)
         out_words = out_1[0].rearrange("p t r -> p (t r)").bitcast(I32)
 
         def listed(idx, t0, n):
             return idx[:, t0 // LIST_ROWS : (t0 + n) // LIST_ROWS]
 
-        def gather_b(t0, n, rows, picked):
-            for k, r in enumerate(rows):
-                nc.vector.tensor_copy(picked[:, k, :], zb[r][:].indirect(listed(idx_b, t0, n)))
+        def gather_b(t0, n, slices, picked):
+            for place, r in enumerate(slices):
+                nc.vector.tensor_copy(picked[:, place, :], zb[r][:].indirect(listed(idx_b, t0, n)))
 
-        def gather_a(t0, n, picked, summed):
+        def gather_a_and_add(t0, n, picked, summed):
             for r in range(PACK):
                 nc.vector.tensor_tensor(summed[:, r, :], za[r][:].indirect(listed(idx_a, t0, n)), picked[r], ADD)
 
-        def relu_round(t0, n, summed, on_vector=False):
-            h_bf = keep.tile([P, n, PACK], BF16, name=f"h_bf{t0}", tag=f"h_bf{t0}", align_bytes=64)
-            if on_vector:
-                nc.vector.tensor_scalar_max(h_bf[:], summed.rearrange("p r t -> p t r"), 0.0)
-            else:
-                nc.scalar.activation(h_bf[:], summed.rearrange("p r t -> p t r"), RELU)
-            return h_bf
+        def rounded_tile(name, n, tag):
+            return keep.tile([P, n, PACK], BF16, name=name, tag=tag, align_bytes=64)
 
-        y_banks = [1, 2, 3, 4, 5]
+        def summed_tile(name, tag):
+            return keep.tile([P, PACK, CHUNK], F32, name=name, tag=tag, align_bytes=64)
 
-        def next_layer(t0, n, h_bf, y, y_bf, on_vector=False):
+        def next_layer(t0, n, h_bf):
             h_w = keep.tile([P, n], U32, name=f"h_w{t0}", align_bytes=64)
             h_s = keep.tile([P, n], U8, name=f"h_s{t0}", align_bytes=64)
             nc.vector.quantize_mx(out=h_w[:].bitcast(FP8X4), scales=h_s[:], in_=h_bf[:].rearrange("p t r -> p (t r)"))
-            acc = psum.tile([P, PACK, n], F32, name=f"y_acc{t0}", tag=f"bank{y_banks.pop(0)}")
+            acc = psum_tile([P, PACK, n], f"y_acc{t0}")
             for r in range(PACK):
                 nc.tensor.matmul_mx(
                     out=acc[:, r, :],
@@ -190,84 +202,86 @@ def tile_moe_combined_hidden_next_layer_pl_kernel(
                     start=True,
                     stop=True,
                 )
-            if on_vector:
-                nc.vector.tensor_copy(y_bf, acc[:].rearrange("p r t -> p t r"))
-            nc.scalar.copy(y, acc[:])
-            if not on_vector:
-                nc.scalar.copy(y_bf, acc[:].rearrange("p r t -> p t r"))
+            return acc
 
-        def store_y(t0, y, queue=nc.sync):
-            queue.dma_start(out=out_rows[:, :, t0 : t0 + STEP], in_=y[:])
+        def store_y(c, acc):
+            y = keep.tile([P, PACK, CHUNK], F32, name=f"y{c}")
+            nc.scalar.copy(y[:], acc[:])
+            nc.sync.dma_start(out=out_rows[:, :, c * CHUNK : (c + 1) * CHUNK], in_=y[:])
 
-        def planes(t0, n, y_bf):
+        def quantise_y(t0, n, y_bf):
             nc.vector.quantize_mx(
                 out=y_w[:, t0 : t0 + n].bitcast(FP8X4),
                 scales=y_s[:, t0 : t0 + n],
                 in_=y_bf[:].rearrange("p t r -> p (t r)"),
             )
-
-        def store_words(t0, n):
             nc.sync.dma_start(out=out_words[:, t0 : t0 + n], in_=y_w[:, t0 : t0 + n].bitcast(I32))
 
-        def summed_tile(t0, n, after):
-            return keep.tile([P, PACK, n], F32, name=f"summed{t0}", tag=after, align_bytes=64)
+        b0_low = keep.tile([P, 1, HALF], F32, name="b0_low", tag="wa_sraw", align_bytes=64)
+        b3_first = shared.tile([P, 1, CHUNK], F32, name="b3_first", offset=3 * CHUNK_BYTES)
+        b3_next = shared.tile([P, 1, HALF], F32, name="b3_next", offset=4 * CHUNK_BYTES)
+        b0_high = shared.tile([P, 1, HALF], F32, name="b0_high", offset=6 * CHUNK_BYTES)
+        b12 = shared.tile([P, 2, EARLY], F32, name="b12", offset=8 * CHUNK_BYTES)
+        gather_b(0, HALF, (0,), b0_low)
+        gather_b(HALF, HALF, (0,), b0_high)
+        gather_b(0, EARLY, (1, 2), b12)
+        gather_b(0, CHUNK, (3,), b3_first)
+        gather_b(CHUNK, HALF, (3,), b3_next)
 
-        y = [keep.tile([P, PACK, STEP], F32, name=f"y{c}") for c in range(4)]
-        y_bf01 = keep.tile([P, HALF, PACK], BF16, name="y_bf01", align_bytes=64)
-        y_bf2 = keep.tile([P, STEP, PACK], BF16, name="y_bf2", align_bytes=64)
-        y_bf3 = keep.tile([P, STEP, PACK], BF16, name="y_bf3", align_bytes=64)
+        def picked_slice_0(t0, n):
+            return b0_low[:, 0, t0 : t0 + n] if t0 < HALF else b0_high[:, 0, t0 - HALF : t0 - HALF + n]
 
-        first = keep.tile([P, 1, HALF], F32, name="picked_first", tag="picked_early", align_bytes=64)
-        rest0 = shared.tile([P, 1, STEP], F32, name="picked_rest0", offset=1536)
-        rest1 = shared.tile([P, 1, 3 * STEP], F32, name="picked_rest1", offset=2048)
-        middle = shared.tile([P, 5, HALF], F32, name="picked_middle", offset=3584)
-        gather_b(0, HALF, (0,), first)
-        gather_b(HALF, HALF, (0,), middle[:, 0:1, :])
-        for r in (1, 2):
-            for half in range(2):
-                gather_b(half * HALF, HALF, (r,), middle[:, 2 * r - 1 + half : 2 * r + half, :])
-        gather_b(0, STEP, (3,), rest0)
-        gather_b(STEP, 3 * STEP, (3,), rest1)
+        def picked_early(c):
+            t0 = c * CHUNK
+            slice_3 = b3_first[:, 0, :] if c == 0 else b3_next[:, 0, t0 - CHUNK : t0]
+            return [picked_slice_0(t0, CHUNK), b12[:, 0, t0 : t0 + CHUNK], b12[:, 1, t0 : t0 + CHUNK], slice_3]
 
-        def picked(t0, n):
-            half, off = divmod(t0, HALF)
-            cols = slice(off, off + n)
-            head = first[:, 0, cols] if half == 0 else middle[:, 0, cols]
-            tail = rest0[:, 0, :] if t0 == 0 else rest1[:, 0, t0 - STEP : t0 - STEP + n]
-            return [head, middle[:, 1 + half, cols], middle[:, 3 + half, cols], tail]
+        def hidden(c, summed):
+            gather_a_and_add(c * CHUNK, CHUNK, picked_early(c), summed[:])
+            h_bf = rounded_tile(f"h_bf{c}", CHUNK, f"h_bf{c}")
+            nc.scalar.activation(h_bf[:], by_token(summed[:]), RELU)
+            return h_bf
 
-        s0 = summed_tile(0, STEP, "summed0")
-        gather_a(0, STEP, picked(0, STEP), s0[:])
-        h0 = relu_round(0, STEP, s0[:])
-        s1 = shared.tile([P, PACK, STEP], F32, name="summed128", offset=0)
-        gather_a(128, STEP, picked(128, STEP), s1[:])
-        h1 = relu_round(128, STEP, s1[:])
-        next_layer(0, STEP, h0, y[0][:], y_bf01[:, 0:STEP, :])
-        store_y(0, y[0])
-        s2 = summed_tile(256, STEP, "h_bf0")
-        gather_a(256, STEP, picked(256, STEP), s2[:])
-        h2 = relu_round(256, STEP, s2[:])
-        next_layer(128, STEP, h1, y[1][:], y_bf01[:, STEP:HALF, :])
-        store_y(128, y[1])
-        s3 = summed_tile(384, 64, "h_bf128")
-        gather_a(384, 64, picked(384, 64), s3[:])
-        next_layer(256, STEP, h2, y[2][:], y_bf2[:])
-        store_y(256, y[2])
-        h3 = relu_round(384, 64, s3[:], on_vector=True)
-        next_layer(384, 64, h3, y[3][:, :, 0:64], y_bf3[:, 0:64, :], on_vector=True)
-        s4 = summed_tile(448, 64, "h_bf256")
-        gather_a(448, 64, picked(448, 64), s4[:])
-        h4 = relu_round(448, 64, s4[:], on_vector=True)
-        next_layer(448, 64, h4, y[3][:, :, 64:STEP], y_bf3[:, 64:STEP, :], on_vector=True)
-        planes(0, HALF, y_bf01)
-        store_words(0, HALF)
-        store_y(384, y[3], nc.scalar)
-        planes(256, STEP, y_bf2)
-        store_words(HALF, STEP)
-        planes(384, STEP, y_bf3)
-        store_words(384, STEP)
+        h0 = hidden(0, summed_tile("summed0", "summed0"))
+        h1 = hidden(1, shared.tile([P, PACK, CHUNK], F32, name="summed1", offset=0))
+        acc0 = next_layer(0, CHUNK, h0)
+        store_y(0, acc0)
+
+        h2 = hidden(2, summed_tile("summed2", "h_bf0"))
+        y_bf01 = rounded_tile("y_bf01", HALF, "h_bf0")
+        nc.scalar.copy(y_bf01[:, 0:CHUNK, :], by_token(acc0[:]))
+        acc1 = next_layer(CHUNK, CHUNK, h1)
+        store_y(1, acc1)
+        nc.scalar.copy(y_bf01[:, CHUNK:HALF, :], by_token(acc1[:]))
+
+        b_late = keep.tile([P, PACK - 1, CHUNK], F32, name="b_late", tag="h_bf1", align_bytes=64)
+        gather_b(EARLY, CHUNK, (1, 2, 3), b_late)
+        acc2 = next_layer(HALF, CHUNK, h2)
+        store_y(2, acc2)
+        y_bf2 = rounded_tile("y_bf2", CHUNK, "y_bf2")
+        nc.scalar.copy(y_bf2[:], by_token(acc2[:]))
+
+        summed3 = summed_tile("summed3", "h_bf2")
+        y3 = keep.tile([P, PACK, CHUNK], F32, name="y3")
+        y_bf3 = rounded_tile("y_bf3", CHUNK, "y_bf3")
+        for c0 in range(0, CHUNK, PIECE):
+            t0 = EARLY + c0
+            cols = slice(c0, c0 + PIECE)
+            picked = [picked_slice_0(t0, PIECE)] + [b_late[:, place, cols] for place in range(PACK - 1)]
+            gather_a_and_add(t0, PIECE, picked, summed3[:, :, cols])
+            h_bf = rounded_tile(f"h_bf_piece{c0}", PIECE, f"h_bf_piece{c0}")
+            nc.vector.tensor_scalar_max(h_bf[:], by_token(summed3[:, :, cols]), 0.0)
+            acc = next_layer(t0, PIECE, h_bf)
+            nc.vector.tensor_copy(y_bf3[:, cols, :], by_token(acc[:]))
+            nc.scalar.copy(y3[:, :, cols], acc[:])
+
+        quantise_y(0, HALF, y_bf01)
+        nc.scalar.dma_start(out=out_rows[:, :, EARLY:WIDTH], in_=y3[:])
+        quantise_y(HALF, CHUNK, y_bf2)
+        quantise_y(EARLY, CHUNK, y_bf3)
+
         for quad in range(QUADS):
-            (nc.sync if quad < 2 else nc.scalar).dma_start(
-                out=out_2[0, 4 * quad : 4 * quad + 4, :].bitcast(I32),
-                in_=y_s[32 * quad : 32 * quad + 4, :].bitcast(I32),
+            queues[quad // 2].dma_start(
+                out=out_2[0, ROWS * quad : ROWS * (quad + 1), :].bitcast(I32),
+                in_=y_s[QUAD * quad : QUAD * quad + ROWS, :].bitcast(I32),
             )

@@ -81,9 +81,9 @@ def tile_moe_combined_hidden_next_layer_pl_kernel(
         wb_s = keep.tile([P, WIDTH], U8, name="wb_s", align_bytes=64)
         xb_w = keep.tile([P, WIDTH], I32, name="xb_w", align_bytes=64)
         xb_s = keep.tile([P, 1, WIDTH], U8, name="xb_s", align_bytes=64)
-        wa_raw = shared.tile([P, PASSES_A, WIDTH], I32, name="wa_raw", offset=2 * CHUNK_BYTES)
+        wa_raw = shared.tile([P, PASSES_A, WIDTH], I32, name="wa_raw", offset=3 * CHUNK_BYTES)
         wa_w = keep.tile([P, PASSES_A, WIDTH], I32, name="wa_w", align_bytes=64)
-        wa_sraw = keep.tile([P, PASSES_A, WIDTH], U8, name="wa_sraw", tag="wa_sraw", align_bytes=64)
+        wa_sraw = keep.tile([P, PASSES_A, WIDTH], U8, name="wa_sraw", align_bytes=64)
         wa_s = keep.tile([P, PASSES_A, WIDTH], U8, name="wa_s", align_bytes=64)
         xa_w = keep.tile([P, PASSES_A, 2 * WIDTH], U8, name="xa_w", align_bytes=64)
         xa_s = keep.tile([P, PASSES_A, WIDTH], U8, name="xa_s", align_bytes=64)
@@ -96,21 +96,23 @@ def tile_moe_combined_hidden_next_layer_pl_kernel(
             nc.vector.memset(plane[:].bitcast(I32), 0)
 
         queues = (nc.sync, nc.scalar)
-        for row in range(ROWS):
+        for row in range(ROWS // 2):
             load_scale_rows_spread(queues[row % 2], wb_sraw, wb_scales, row)
-        for quad in range(QUADS // 2):
-            load_scale_rows(queues[quad % 2], xb_s, xb_scales, quad)
         nc.sync.dma_start(out=wb_raw[:].bitcast(I32), in_=wb_words[0].bitcast(I32))
+        for row in range(ROWS // 2, ROWS):
+            load_scale_rows_spread(queues[(row + 1) % 2], wb_sraw, wb_scales, row)
+        for quad in range(QUADS // 2):
+            load_scale_rows(queues[(quad + 1) % 2], xb_s, xb_scales, quad)
         nc.scalar.dma_start(out=xb_w[:], in_=xb_words[0].rearrange("p n t -> p (n t)").bitcast(I32))
         for quad in range(QUADS // 2, QUADS):
             load_scale_rows(queues[quad % 2], xb_s, xb_scales, quad)
+        nc.sync.dma_start(out=wa_raw[:], in_=wa_words.rearrange("g p n t -> p g (n t)").bitcast(I32))
         nc.sync.dma_start(idx_b[:], offs2)
         for quad in range(QUADS):
             load_scale_rows(nc.sync, wa_sraw, wa_scales, quad)
-        nc.sync.dma_start(out=wa_raw[:], in_=wa_words.rearrange("g p n t -> p g (n t)").bitcast(I32))
+        nc.sync.dma_start(out=xa_w[:].bitcast(I32), in_=xa_words.rearrange("g p c -> p g c").bitcast(I32))
         for quad in range(QUADS):
             load_scale_rows(nc.sync, xa_s, xa_scales, quad)
-        nc.sync.dma_start(out=xa_w[:].bitcast(I32), in_=xa_words.rearrange("g p c -> p g c").bitcast(I32))
         nc.sync.dma_start(idx_a[:], offs)
         nc.sync.dma_start(out=wm_raw[:], in_=wm_words[0].rearrange("p n t -> p (n t)").bitcast(I32))
         for quad in range(QUADS):
@@ -142,8 +144,8 @@ def tile_moe_combined_hidden_next_layer_pl_kernel(
                 nc.scalar.copy(table[:, c0 : c0 + width], acc[:])
             zb.append(table)
 
-        deal(nc.vector, wa_s[:], wa_sraw[:], 1)
         deal(nc.vector, wa_w[:], wa_raw[:], 4)
+        deal(nc.gpsimd, wa_s[:], wa_sraw[:], 1)
 
         za = []
         for r in range(PACK):
@@ -217,11 +219,11 @@ def tile_moe_combined_hidden_next_layer_pl_kernel(
             )
             nc.sync.dma_start(out=out_words[:, t0 : t0 + n], in_=y_w[:, t0 : t0 + n].bitcast(I32))
 
-        b0_low = keep.tile([P, 1, HALF], F32, name="b0_low", tag="wa_sraw", align_bytes=64)
         b3_first = shared.tile([P, 1, CHUNK], F32, name="b3_first", offset=3 * CHUNK_BYTES)
         b3_next = shared.tile([P, 1, HALF], F32, name="b3_next", offset=4 * CHUNK_BYTES)
         b0_high = shared.tile([P, 1, HALF], F32, name="b0_high", offset=6 * CHUNK_BYTES)
-        b12 = shared.tile([P, 2, EARLY], F32, name="b12", offset=8 * CHUNK_BYTES)
+        b0_low = shared.tile([P, 1, HALF], F32, name="b0_low", offset=8 * CHUNK_BYTES)
+        b12 = shared.tile([P, 2, EARLY], F32, name="b12", offset=10 * CHUNK_BYTES)
         gather_b(0, HALF, (0,), b0_low)
         gather_b(HALF, HALF, (0,), b0_high)
         gather_b(0, EARLY, (1, 2), b12)

from contextlib import ExitStack

import concourse.mybir as mybir

F32 = mybir.dt.float32
BF16 = mybir.dt.bfloat16
I32 = mybir.dt.int32
U32 = mybir.dt.uint32
U16 = mybir.dt.uint16
U8 = mybir.dt.uint8
FP8X4 = mybir.dt.float8_e4m3fn_x4
FP4X4 = mybir.dt.float4_e2m1fn_x4
RELU = mybir.ActivationFunctionType.Relu
ADD = mybir.AluOpType.add

P = 128
PACK = 4
WIDTH = 512
PASSES_A = 2
QUADS = 4
QUAD = P // QUADS
ROWS = 4
LIST_ROWS = 16
LINE = 16
BANKS = 8
CHUNK = 128
HALF = 2 * CHUNK
PIECE = CHUNK // 2
EARLY = 3 * CHUNK
CHUNK_BYTES = 4 * CHUNK

FLOPS = 2 * WIDTH * WIDTH * (PASSES_A * WIDTH + WIDTH + WIDTH)


def load_scale_rows(queue, plane, scales, quad):
    queue.dma_start(
        out=plane[QUAD * quad : QUAD * quad + ROWS].bitcast(I32),
        in_=scales[:, ROWS * quad : ROWS * (quad + 1), :].rearrange("g q c -> q g c").bitcast(I32),
    )


def load_scale_rows_spread(queue, plane, scales, row):
    queue.dma_start(
        out=plane[row:P:ROWS, 0, :].bitcast(I32),
        in_=scales[0, row : QUADS * ROWS : ROWS, :]
        .bitcast(I32)
        .unsqueeze(1)
        .to_broadcast([QUADS, QUAD // ROWS, WIDTH // 4]),
    )


def deal(engine, dealt, raw, item_bytes):
    run = LINE // item_bytes
    engine.tensor_copy(
        out=dealt.rearrange("p g (r c i) -> p g c r i", r=PACK, i=run),
        in_=raw.rearrange("p g (c i r) -> p g c r i", r=PACK, i=run),
    )


def by_token(slices):
    return slices.rearrange("p r t -> p t r")


def tile_moe_combined_hidden_next_layer_pl_kernel(
    tc, xa_words, xa_scales, wa_words, wa_scales, xb_words, xb_scales, wb_words, wb_scales,
    wm_words, wm_scales, offs, offs2, out_0, out_1, out_2,
):
    nc = tc.nc
    with ExitStack() as ctx:
        lists = ctx.enter_context(tc.tile_pool(name="lists", bufs=1))
        keep = ctx.enter_context(tc.tile_pool(name="keep", bufs=1))
        shared = ctx.enter_context(tc.tile_pool(name="shared", bufs=1))
        psum = ctx.enter_context(tc.psum_pool(name="psum", bufs=1))

        idx_a = lists.tile([P, WIDTH // LIST_ROWS], U16, name="idx_a")
        idx_b = lists.tile([P, WIDTH // LIST_ROWS], U16, name="idx_b")

        wb_raw = keep.tile([P, 2 * WIDTH], U8, name="wb_raw", align_bytes=64)
        wb_w = keep.tile([P, 2 * WIDTH], U8, name="wb_w", align_bytes=64)
        wb_sraw = keep.tile([P, 1, WIDTH], U8, name="wb_sraw", align_bytes=64)
        wb_s = keep.tile([P, WIDTH], U8, name="wb_s", align_bytes=64)
        xb_w = keep.tile([P, WIDTH], I32, name="xb_w", align_bytes=64)
        xb_s = keep.tile([P, 1, WIDTH], U8, name="xb_s", align_bytes=64)
        wa_raw = shared.tile([P, PASSES_A, WIDTH], I32, name="wa_raw", offset=3 * CHUNK_BYTES)
        wa_w = keep.tile([P, PASSES_A, WIDTH], I32, name="wa_w", align_bytes=64)
        wa_sraw = keep.tile([P, PASSES_A, WIDTH], U8, name="wa_sraw", align_bytes=64)
        wa_s = keep.tile([P, PASSES_A, WIDTH], U8, name="wa_s", align_bytes=64)
        xa_w = keep.tile([P, PASSES_A, 2 * WIDTH], U8, name="xa_w", align_bytes=64)
        xa_s = keep.tile([P, PASSES_A, WIDTH], U8, name="xa_s", align_bytes=64)
        wm_raw = keep.tile([P, WIDTH], I32, name="wm_raw", align_bytes=64)
        wm_w = keep.tile([P, WIDTH], I32, name="wm_w", align_bytes=64)
        wm_sraw = keep.tile([P, 1, WIDTH], U8, name="wm_sraw", align_bytes=64)
        wm_s = keep.tile([P, WIDTH], U8, name="wm_s", align_bytes=64)

        for plane in (xb_s, wa_sraw, xa_s, wm_sraw):
            nc.vector.memset(plane[:].bitcast(I32), 0)

        queues = (nc.sync, nc.scalar)
        for row in range(ROWS // 2):
            load_scale_rows_spread(queues[row % 2], wb_sraw, wb_scales, row)
        nc.sync.dma_start(out=wb_raw[:].bitcast(I32), in_=wb_words[0].bitcast(I32))
        for row in range(ROWS // 2, ROWS):
            load_scale_rows_spread(queues[(row + 1) % 2], wb_sraw, wb_scales, row)
        for quad in range(QUADS // 2):
            load_scale_rows(queues[(quad + 1) % 2], xb_s, xb_scales, quad)
        nc.scalar.dma_start(out=xb_w[:], in_=xb_words[0].rearrange("p n t -> p (n t)").bitcast(I32))
        for quad in range(QUADS // 2, QUADS):
            load_scale_rows(queues[quad % 2], xb_s, xb_scales, quad)
        nc.sync.dma_start(out=wa_raw[:], in_=wa_words.rearrange("g p n t -> p g (n t)").bitcast(I32))
        nc.sync.dma_start(idx_b[:], offs2)
        for quad in range(QUADS):
            load_scale_rows(nc.sync, wa_sraw, wa_scales, quad)
        nc.sync.dma_start(out=xa_w[:].bitcast(I32), in_=xa_words.rearrange("g p c -> p g c").bitcast(I32))
        for quad in range(QUADS):
            load_scale_rows(nc.sync, xa_s, xa_scales, quad)
        nc.sync.dma_start(idx_a[:], offs)
        nc.sync.dma_start(out=wm_raw[:], in_=wm_words[0].rearrange("p n t -> p (n t)").bitcast(I32))
        for quad in range(QUADS):
            load_scale_rows(nc.sync, wm_sraw, wm_scales, quad)

        bank_turn = list(range(2 * BANKS))

        def psum_tile(shape, name):
            return psum.tile(shape, F32, name=name, tag=f"bank{bank_turn.pop(0) % BANKS}")

        deal(nc.vector, wb_w[:].bitcast(U16).unsqueeze(1), wb_raw[:].bitcast(U16).unsqueeze(1), 2)
        deal(nc.vector, wb_s[:].unsqueeze(1), wb_sraw[:], 1)

        zb = []
        for r in range(PACK):
            table = keep.tile([P, WIDTH], F32, name=f"zb{r}")
            width = HALF if r == 0 else WIDTH
            for c0 in range(0, WIDTH, width):
                acc = psum_tile([P, width], f"zb_acc{r}_{c0}")
                nc.tensor.matmul_mx(
                    out=acc[:],
                    lhsT=wb_w[:, 2 * P * r : 2 * P * (r + 1)].bitcast(FP4X4),
                    lhsT_scale=wb_s[:, P * r : P * (r + 1)],
                    rhs=xb_w[:, c0 : c0 + width].bitcast(FP8X4),
                    rhs_scale=xb_s[:, 0, c0 : c0 + width],
                    start=True,
                    stop=True,
                )
                nc.scalar.copy(table[:, c0 : c0 + width], acc[:])
            zb.append(table)

        deal(nc.vector, wa_w[:], wa_raw[:], 4)
        deal(nc.gpsimd, wa_s[:], wa_sraw[:], 1)

        za = []
        for r in range(PACK):
            acc = psum_tile([P, WIDTH], f"za_acc{r}")
            for g in range(PASSES_A):
                nc.tensor.matmul_mx(
                    out=acc[:],
                    lhsT=wa_w[:, g, P * r : P * (r + 1)].bitcast(FP8X4),
                    lhsT_scale=wa_s[:, g, P * r : P * (r + 1)],
                    rhs=xa_w[:, g, :].bitcast(FP4X4),
                    rhs_scale=xa_s[:, g, :],
                    start=(g == 0),
                    stop=(g == PASSES_A - 1),
                )
            table = keep.tile([P, WIDTH], F32, name=f"za{r}")
            nc.scalar.copy(table[:], acc[:])
            za.append(table)

        deal(nc.gpsimd, wm_w[:].unsqueeze(1), wm_raw[:].unsqueeze(1), 4)
        deal(nc.gpsimd, wm_s[:].unsqueeze(1), wm_sraw[:], 1)

        y_w = keep.tile([P, WIDTH], U32, name="y_w", align_bytes=64)
        y_s = keep.tile([P, WIDTH], U8, name="y_s", align_bytes=64)
        out_rows = out_0.rearrange("(p r) t -> p r t", r=PACK)
        out_words = out_1[0].rearrange("p t r -> p (t r)").bitcast(I32)

        def listed(idx, t0, n):
            return idx[:, t0 // LIST_ROWS : (t0 + n) // LIST_ROWS]

        def gather_b(t0, n, slices, picked):
            for place, r in enumerate(slices):
                nc.vector.tensor_copy(picked[:, place, :], zb[r][:].indirect(listed(idx_b, t0, n)))

        def gather_a_and_add(t0, n, picked, summed):
            for r in range(PACK):
                nc.vector.tensor_tensor(summed[:, r, :], za[r][:].indirect(listed(idx_a, t0, n)), picked[r], ADD)

        def rounded_tile(name, n, tag):
            return keep.tile([P, n, PACK], BF16, name=name, tag=tag, align_bytes=64)

        def summed_tile(name, tag):
            return keep.tile([P, PACK, CHUNK], F32, name=name, tag=tag, align_bytes=64)

        def next_layer(t0, n, h_bf):
            h_w = keep.tile([P, n], U32, name=f"h_w{t0}", align_bytes=64)
            h_s = keep.tile([P, n], U8, name=f"h_s{t0}", align_bytes=64)
            nc.vector.quantize_mx(out=h_w[:].bitcast(FP8X4), scales=h_s[:], in_=h_bf[:].rearrange("p t r -> p (t r)"))
            acc = psum_tile([P, PACK, n], f"y_acc{t0}")
            for r in range(PACK):
                nc.tensor.matmul_mx(
                    out=acc[:, r, :],
                    lhsT=wm_w[:, P * r : P * (r + 1)].bitcast(FP8X4),
                    lhsT_scale=wm_s[:, P * r : P * (r + 1)],
                    rhs=h_w[:].bitcast(FP8X4),
                    rhs_scale=h_s[:],
                    start=True,
                    stop=True,
                )
            return acc

        def store_y(c, acc):
            y = keep.tile([P, PACK, CHUNK], F32, name=f"y{c}")
            nc.scalar.copy(y[:], acc[:])
            nc.sync.dma_start(out=out_rows[:, :, c * CHUNK : (c + 1) * CHUNK], in_=y[:])

        def quantise_y(t0, n, y_bf):
            nc.vector.quantize_mx(
                out=y_w[:, t0 : t0 + n].bitcast(FP8X4),
                scales=y_s[:, t0 : t0 + n],
                in_=y_bf[:].rearrange("p t r -> p (t r)"),
            )
            nc.sync.dma_start(out=out_words[:, t0 : t0 + n], in_=y_w[:, t0 : t0 + n].bitcast(I32))

        b3_first = shared.tile([P, 1, CHUNK], F32, name="b3_first", offset=3 * CHUNK_BYTES)
        b3_next = shared.tile([P, 1, HALF], F32, name="b3_next", offset=4 * CHUNK_BYTES)
        b0_high = shared.tile([P, 1, HALF], F32, name="b0_high", offset=6 * CHUNK_BYTES)
        b0_low = shared.tile([P, 1, HALF], F32, name="b0_low", offset=8 * CHUNK_BYTES)
        b12 = shared.tile([P, 2, EARLY], F32, name="b12", offset=10 * CHUNK_BYTES)
        gather_b(0, HALF, (0,), b0_low)
        gather_b(HALF, HALF, (0,), b0_high)
        gather_b(0, EARLY, (1, 2), b12)
        gather_b(0, CHUNK, (3,), b3_first)
        gather_b(CHUNK, HALF, (3,), b3_next)

        def picked_slice_0(t0, n):
            return b0_low[:, 0, t0 : t0 + n] if t0 < HALF else b0_high[:, 0, t0 - HALF : t0 - HALF + n]

        def picked_early(c):
            t0 = c * CHUNK
            slice_3 = b3_first[:, 0, :] if c == 0 else b3_next[:, 0, t0 - CHUNK : t0]
            return [picked_slice_0(t0, CHUNK), b12[:, 0, t0 : t0 + CHUNK], b12[:, 1, t0 : t0 + CHUNK], slice_3]

        def hidden(c, summed):
            gather_a_and_add(c * CHUNK, CHUNK, picked_early(c), summed[:])
            h_bf = rounded_tile(f"h_bf{c}", CHUNK, f"h_bf{c}")
            nc.scalar.activation(h_bf[:], by_token(summed[:]), RELU)
            return h_bf

        h0 = hidden(0, summed_tile("summed0", "summed0"))
        h1 = hidden(1, shared.tile([P, PACK, CHUNK], F32, name="summed1", offset=0))
        acc0 = next_layer(0, CHUNK, h0)
        store_y(0, acc0)

        h2 = hidden(2, summed_tile("summed2", "h_bf0"))
        y_bf01 = rounded_tile("y_bf01", HALF, "h_bf0")
        nc.scalar.copy(y_bf01[:, 0:CHUNK, :], by_token(acc0[:]))
        acc1 = next_layer(CHUNK, CHUNK, h1)
        store_y(1, acc1)
        nc.scalar.copy(y_bf01[:, CHUNK:HALF, :], by_token(acc1[:]))

        b_late = keep.tile([P, PACK - 1, CHUNK], F32, name="b_late", tag="h_bf1", align_bytes=64)
        gather_b(EARLY, CHUNK, (1, 2, 3), b_late)
        acc2 = next_layer(HALF, CHUNK, h2)
        store_y(2, acc2)
        y_bf2 = rounded_tile("y_bf2", CHUNK, "y_bf2")
        nc.scalar.copy(y_bf2[:], by_token(acc2[:]))

        summed3 = summed_tile("summed3", "h_bf2")
        y3 = keep.tile([P, PACK, CHUNK], F32, name="y3")
        y_bf3 = rounded_tile("y_bf3", CHUNK, "y_bf3")
        for c0 in range(0, CHUNK, PIECE):
            t0 = EARLY + c0
            cols = slice(c0, c0 + PIECE)
            picked = [picked_slice_0(t0, PIECE)] + [b_late[:, place, cols] for place in range(PACK - 1)]
            gather_a_and_add(t0, PIECE, picked, summed3[:, :, cols])
            h_bf = rounded_tile(f"h_bf_piece{c0}", PIECE, f"h_bf_piece{c0}")
            nc.vector.tensor_scalar_max(h_bf[:], by_token(summed3[:, :, cols]), 0.0)
            acc = next_layer(t0, PIECE, h_bf)
            nc.vector.tensor_copy(y_bf3[:, cols, :], by_token(acc[:]))
            nc.scalar.copy(y3[:, :, cols], acc[:])

        quantise_y(0, HALF, y_bf01)
        nc.scalar.dma_start(out=out_rows[:, :, EARLY:WIDTH], in_=y3[:])
        quantise_y(HALF, CHUNK, y_bf2)
        quantise_y(EARLY, CHUNK, y_bf3)

        for quad in range(QUADS):
            queues[quad // 2].dma_start(
                out=out_2[0, ROWS * quad : ROWS * (quad + 1), :].bitcast(I32),
                in_=y_s[QUAD * quad : QUAD * quad + ROWS, :].bitcast(I32),
            )
